import numpy as np
import ml_dtypes


def mxq(x, axis, fmt="e4m3"):
    dtype, down = {"e4m3": (ml_dtypes.float8_e4m3fn, 7), "e5m2": (ml_dtypes.float8_e5m2, 14)}[fmt]
    v = np.moveaxis(np.asarray(x, np.float32).astype(ml_dtypes.bfloat16).astype(np.float64), axis, -1)
    blocks = v.reshape(v.shape[:-1] + (-1, 32))
    amax = np.abs(blocks).max(-1, keepdims=True)
    byte = np.maximum(np.where(amax > 0, np.frexp(amax)[1] - 1 + 127, 0) - down, 1)
    scale = np.exp2(byte - 127.0)
    codes = (blocks / scale).astype(np.float32).astype(dtype).astype(np.float64)
    return np.moveaxis((codes * scale).reshape(v.shape), -1, axis)


WIDE = False


def mx_kscale(k):
    if not WIDE:
        return np.ones(k)
    levels = np.array([10, -10, 5, -5, 0])
    if k % 512:
        return np.exp2(np.random.permutation(np.resize(levels, k // 32))).repeat(32)
    a = np.empty((k // 512, 16))
    for p in range(k // 512):
        a[p, :8] = np.random.permutation(np.resize(levels, 8))
        for g in range(8):
            far = levels[np.abs(levels - a[p, g]) >= 10]
            a[p, g + 8] = far[np.random.randint(len(far))]
    return np.exp2(a.ravel()).repeat(32)


def f64(x):
    return np.asarray(x).astype(np.float64)


def striped(idx):
    return np.tile(idx.reshape(-1, 16).T, (8, 1)).astype(np.uint16)


def unstriped(offs):
    return offs[:16].T.reshape(-1).astype(np.int64)


def pack_weight(w):
    k, n = w.shape
    w = f64(np.asarray(w, np.float32).astype(ml_dtypes.bfloat16)).reshape(k // 32, 32, n)
    amax = np.abs(w).max(1)
    byte = np.clip(np.where(amax > 0, np.frexp(amax)[1] - 1 + 127 - 7, 1), 1, 254)
    scaled = (w * np.exp2(127.0 - byte)[:, None, :]).reshape(k, n).astype(np.float32)
    words = np.ascontiguousarray(scaled.reshape(k // 512, 128, 4, n).transpose(0, 1, 3, 2)).astype(ml_dtypes.float8_e4m3fn).view(np.uint8)
    return words, np.ascontiguousarray(byte.astype(np.uint8).reshape(k // 512, 16, n))


def unpack_weight(words, scales):
    g, p, n, _ = words.shape
    vals = np.ascontiguousarray(words).view(ml_dtypes.float8_e4m3fn).astype(np.float64) * np.repeat(np.exp2(scales.astype(np.float64) - 127.0), 8, axis=1)[..., None]
    return vals.transpose(0, 1, 3, 2).reshape(g * 512, n)


K, T, S, N, H, V = 512, 1024, 512, 128, 512, 256


def setup_inputs():
    n = np.random.standard_normal
    s = mx_kscale(K)[:, None]
    u = mx_kscale(H)
    packed_xT = pack_weight(n((K, T)) * s)
    return {
        "x_words": packed_xT[0],
        "x_scales": packed_xT[1],
        "w1": (n((K, H)) / np.sqrt(K) / s).astype(np.float32),
        "w2": (n((K, H)) / np.sqrt(K) / s).astype(np.float32),
        "tgt": (n((H, V))).astype(np.float32),
        "probe": (np.random.uniform(0.4, 1.6, (H, S))).astype(np.float32),
        "unit": (np.random.uniform(0.6, 1.4, (H, 1)) * u[:, None]).astype(np.float32),
        "w3": (n((H, N)) / np.sqrt(H) / u[:, None]).astype(np.float32),
        "offs": striped(np.random.permutation(T)[:S]),
        "ed": striped(np.random.permutation(S)[:V]),
        "hit": striped(np.random.permutation(S)[:V]),
    }


def reference(x_words, x_scales, w1, w2, tgt, probe, unit, w3, offs, ed, hit):
    xq = unpack_weight(x_words, x_scales)[:, unstriped(offs)]
    yv = mxq(f64(w2), 0, "e4m3").T @ xq
    y = mxq(f64(w1), 0, "e4m3").T @ xq
    key_ = y[:, unstriped(ed)]
    match = (key_ * y[:, unstriped(hit)]) / ((key_) ** 2 + 0.6)
    resd = f64(tgt) - yv[:, unstriped(ed)]
    delta = (0.9 * np.tanh(match)) * resd
    vn = yv[:, unstriped(hit)] + delta
    vnew = yv.copy()
    vnew[:, unstriped(hit)] = vn
    prb = vnew * f64(probe)
    hid = f64(unit) * prb
    return mxq(f64(w3), 0, "e4m3").T @ mxq(hid, 0, "e4m3")

@@ -1,0 +1,220 @@
+from contextlib import ExitStack
+
+import concourse.mybir as mybir
+
+K, T, S, N, H, V = 512, 1024, 512, 128, 512, 256
+FLOPS = 2 * K * H * S * 2 + 2 * H * N * S
+
+F32 = mybir.dt.float32
+BF16 = mybir.dt.bfloat16
+I32 = mybir.dt.int32
+U32 = mybir.dt.uint32
+U16 = mybir.dt.uint16
+U8 = mybir.dt.uint8
+FP8X4 = mybir.dt.float8_e4m3fn_x4
+ACT = mybir.ActivationFunctionType
+ALU = mybir.AluOpType
+
+P = 128
+PACK = 4
+HALF = H // 2
+
+
+def tile_picked_yeditm_prob_p_kernel(
+    tc, x_words, x_scales, w1, w2, tgt, probe, unit, w3, offs, ed, hit, out
+):
+    nc = tc.nc
+    with ExitStack() as ctx:
+        keep = ctx.enter_context(tc.tile_pool(name="keep", bufs=1))
+        psum = ctx.enter_context(tc.psum_pool(name="psum", bufs=1))
+
+        offs_sb = keep.tile([P, S // 16], U16, name="offs_sb")
+        ed_sb = keep.tile([P, V // 16], U16, name="ed_sb")
+        hit_sb = keep.tile([P, V // 16], U16, name="hit_sb")
+        words = keep.tile([P, T], U32, name="words", align_bytes=64)
+        planes = keep.tile([P, T], U8, name="planes", align_bytes=64)
+
+        nc.gpsimd.memset(planes[:].bitcast(I32), 0)
+        nc.sync.dma_start(offs_sb[:], offs)
+        nc.sync.dma_start(words[:].bitcast(I32), x_words[0].rearrange("p n t -> p (n t)").bitcast(I32))
+        for q in range(4):
+            nc.scalar.dma_start(
+                planes[32 * q : 32 * q + 4, :].bitcast(I32), x_scales[0, 4 * q : 4 * q + 4, :].bitcast(I32)
+            )
+
+        def load_halves(w, name):
+            rows = w.rearrange("(p j) c -> p j c", j=PACK)
+            halves = []
+            for h in range(2):
+                raw = keep.tile([P, PACK, HALF], F32, name=f"{name}_raw{h}")
+                nc.sync.dma_start(raw[:], rows[:, :, h * HALF : (h + 1) * HALF])
+                halves.append(raw)
+            return halves
+
+        w1_raw = load_halves(w1, "w1")
+        nc.sync.dma_start(ed_sb[:], ed)
+        nc.sync.dma_start(hit_sb[:], hit)
+        w2_raw = load_halves(w2, "w2")
+        tgt_sb = keep.tile([P, PACK, V], F32, name="tgt_sb")
+        nc.sync.dma_start(tgt_sb[:], tgt.rearrange("(p t) v -> p t v", t=PACK))
+        w3_raw = keep.tile([P, PACK, N], F32, name="w3_raw")
+        nc.sync.dma_start(w3_raw[:], w3.rearrange("(p j) c -> p j c", j=PACK))
+        unit_sb = keep.tile([P, PACK], F32, name="unit_sb")
+        nc.sync.dma_start(unit_sb[:], unit.rearrange("(p t) o -> p (t o)", t=PACK))
+        probe_sb = keep.tile([P, PACK, S], F32, name="probe_sb")
+        nc.sync.dma_start(probe_sb[:], probe.rearrange("(p t) s -> p t s", t=PACK))
+
+        x_codes = keep.tile([P, S], U32, name="x_codes", align_bytes=64)
+        x_plane = keep.tile([P, S], U8, name="x_plane", align_bytes=64)
+        nc.vector.tensor_copy(x_plane[:], planes[:].indirect(offs_sb[:]))
+        nc.vector.tensor_copy(x_codes[:], words[:].indirect(offs_sb[:]))
+
+        def deal(copy, grouped, raw, h):
+            m0 = h * HALF // PACK
+            copy(
+                grouped[:, :, m0 : m0 + HALF // PACK, :].rearrange("p t m j -> p m j t"),
+                raw[:].rearrange("p j (m t) -> p m j t", t=PACK),
+            )
+
+        def quantize(codes, plane, grouped, t0, t1):
+            nc.vector.quantize_mx(
+                out=codes[:, t0 * P : t1 * P].bitcast(FP8X4),
+                scales=plane[:, t0 * P : t1 * P],
+                in_=grouped[:, t0:t1].rearrange("p t m j -> p (t m j)"),
+            )
+
+        def product(codes, plane, t, bank):
+            acc = psum.tile([P, S], F32, name=f"bank{bank}")
+            nc.tensor.matmul_mx(
+                out=acc[:],
+                lhsT=codes[:, t * P : (t + 1) * P].bitcast(FP8X4),
+                lhsT_scale=plane[:, t * P : (t + 1) * P],
+                rhs=x_codes[:].bitcast(FP8X4),
+                rhs_scale=x_plane[:],
+                start=True,
+                stop=True,
+            )
+            return acc
+
+        w1_bf = keep.tile([P, PACK, P, PACK], BF16, name="w1_bf", align_bytes=64)
+        w1_codes = keep.tile([P, H], U32, name="w1_codes", align_bytes=64)
+        w1_plane = keep.tile([P, H], U8, name="w1_plane", align_bytes=64)
+        deal(nc.scalar.copy, w1_bf, w1_raw[0], 0)
+        deal(nc.vector.tensor_copy, w1_bf, w1_raw[1], 1)
+        quantize(w1_codes, w1_plane, w1_bf, 0, 1)
+        quantize(w1_codes, w1_plane, w1_bf, 1, 4)
+        y_acc = [product(w1_codes, w1_plane, t, t) for t in range(PACK)]
+
+        w2_bf = keep.tile([P, PACK, P, PACK], BF16, name="w2_bf", align_bytes=64)
+        w2_codes = keep.tile([P, H], U32, name="w2_codes", align_bytes=64)
+        w2_plane = keep.tile([P, H], U8, name="w2_plane", align_bytes=64)
+        deal(nc.scalar.copy, w2_bf, w2_raw[0], 0)
+
+        y = [keep.tile([P, S], F32, name=f"y{t}") for t in range(PACK)]
+        yv = [keep.tile([P, S], F32, name=f"yv{t}") for t in range(PACK)]
+        key = keep.tile([P, PACK, V], F32, name="key")
+        sq = keep.tile([P, PACK, PACK, V // PACK], F32, name="sq")
+        lg = keep.tile([P, PACK, V], F32, name="lg")
+        num = keep.tile([P, PACK, V], F32, name="num")
+        miss = keep.tile([P, PACK, V], F32, name="miss")
+
+        def keys(t):
+            sq_t = sq[:, t].rearrange("p c v -> p (c v)")
+            nc.scalar.copy(y[t][:], y_acc[t][:])
+            if t == 0:
+                nc.vector.tensor_copy(key[:, t, :], y[t][:].indirect(ed_sb[:]))
+                nc.vector.tensor_tensor(sq_t, key[:, t, :], key[:, t, :], ALU.mult)
+            else:
+                nc.scalar.activation(key[:, t, :], y[t][:].indirect(ed_sb[:]), ACT.Copy)
+                nc.scalar.activation(sq_t, key[:, t, :], ACT.Square)
+            nc.scalar.activation(lg[:, t, :], sq_t, ACT.Ln, bias=0.6)
+
+        keys(0)
+        deal(nc.vector.tensor_copy, w2_bf, w2_raw[1], 1)
+        quantize(w2_codes, w2_plane, w2_bf, 0, 4)
+        yv_acc = [product(w2_codes, w2_plane, t, PACK + t) for t in range(PACK)]
+        for t in range(1, PACK):
+            keys(t)
+        for t in range(PACK):
+            nc.vector.tensor_tensor(num[:, t, :], y[t][:].indirect(hit_sb[:]), key[:, t, :], ALU.mult)
+            nc.vector.tensor_copy(yv[t][:], yv_acc[t][:])
+            nc.vector.tensor_tensor(miss[:, t, :], yv[t][:].indirect(ed_sb[:]), tgt_sb[:, t, :], ALU.subtract)
+
+        w3_bf = keep.tile([P, N, PACK], BF16, name="w3_bf", align_bytes=64)
+        w3_codes = keep.tile([P, N], U32, name="w3_codes", align_bytes=64)
+        w3_plane = keep.tile([P, N], U8, name="w3_plane", align_bytes=64)
+        nc.vector.tensor_copy(
+            w3_bf[:].rearrange("p (c i) j -> p c j i", i=4), w3_raw[:].rearrange("p j (c i) -> p c j i", i=4)
+        )
+        nc.vector.quantize_mx(
+            out=w3_codes[:].bitcast(FP8X4), scales=w3_plane[:], in_=w3_bf[:].rearrange("p c j -> p (c j)")
+        )
+
+        match = keep.tile([P, PACK, V], F32, name="match")
+        bound = keep.tile([P, PACK, V], F32, name="bound")
+        delta = keep.tile([P, PACK, V], F32, name="delta")
+        vn = keep.tile([P, PACK, V], F32, name="vn")
+        hid = keep.tile([P, PACK, S], BF16, name="hid")
+
+        def bounded_match(t):
+            rec_t = sq[:, :, t, :]
+            nc.scalar.activation(rec_t, lg[:, t, :].rearrange("p (c v) -> p c v", c=PACK), ACT.Exp, scale=-1.0)
+            nc.vector.tensor_tensor(
+                match[:, t, :].rearrange("p (c v) -> p c v", c=PACK),
+                num[:, t, :].rearrange("p (c v) -> p c v", c=PACK),
+                rec_t,
+                ALU.mult,
+            )
+            nc.scalar.activation(bound[:, t, :], match[:, t, :], ACT.Tanh)
+
+        def edit_store(t):
+            nc.vector.scalar_tensor_tensor(delta[:, t, :], bound[:, t, :], -0.9, miss[:, t, :], ALU.mult, ALU.mult)
+            if t < PACK - 1:
+                nc.vector.tensor_tensor(vn[:, t, :], yv[t][:].indirect(hit_sb[:]), delta[:, t, :], ALU.add)
+                nc.scalar.activation(yv[t][:].indirect(hit_sb[:]), vn[:, t, :], ACT.Copy)
+            else:
+                nc.scalar.activation(vn[:, t, :], yv[t][:].indirect(hit_sb[:]), ACT.Copy)
+                nc.vector.tensor_tensor(yv[t][:].indirect(hit_sb[:]), vn[:, t, :], delta[:, t, :], ALU.add)
+
+        def read_store(t):
+            nc.vector.scalar_tensor_tensor(
+                hid[:, t, :], yv[t][:], unit_sb[:, t : t + 1], probe_sb[:, t, :], ALU.mult, ALU.mult
+            )
+
+        for t in range(PACK):
+            bounded_match(t)
+        for t in range(PACK):
+            edit_store(t)
+        for t in range(PACK):
+            read_store(t)
+
+        hid_bf = keep.tile([P, S, PACK], BF16, name="hid_bf", align_bytes=64)
+        hid_codes = keep.tile([P, S], U32, name="hid_codes", align_bytes=64)
+        hid_plane = keep.tile([P, S], U8, name="hid_plane", align_bytes=64)
+        result = keep.tile([P, S], F32, name="result")
+        half = S // 2
+        for h, copy in ((0, nc.scalar.copy), (1, nc.vector.tensor_copy)):
+            cols = slice(h * half, (h + 1) * half)
+            copy(
+                hid_bf[:, cols, :].rearrange("p (c i) t -> p c t i", i=4),
+                hid[:, :, cols].rearrange("p t (c i) -> p c t i", i=4),
+            )
+        for h, copy in ((1, nc.scalar.copy), (0, nc.vector.tensor_copy)):
+            cols = slice(h * half, (h + 1) * half)
+            nc.vector.quantize_mx(
+                out=hid_codes[:, cols].bitcast(FP8X4),
+                scales=hid_plane[:, cols],
+                in_=hid_bf[:, cols, :].rearrange("p c t -> p (c t)"),
+            )
+            acc = psum.tile([P, S], F32, name=f"bank{h}")
+            nc.tensor.matmul_mx(
+                out=acc[:, :half],
+                lhsT=w3_codes[:].bitcast(FP8X4),
+                lhsT_scale=w3_plane[:],
+                rhs=hid_codes[:, cols].bitcast(FP8X4),
+                rhs_scale=hid_plane[:, cols],
+                start=True,
+                stop=True,
+            )
+            copy(result[:, cols], acc[:, :half])
+            nc.sync.dma_start(out[:, cols], result[:, cols])

@@ -26,6 +26,7 @@ def tile_picked_yeditm_prob_p_kernel(
     nc = tc.nc
     with ExitStack() as ctx:
         keep = ctx.enter_context(tc.tile_pool(name="keep", bufs=1))
+        reuse = ctx.enter_context(tc.tile_pool(name="reuse", bufs=1))
         psum = ctx.enter_context(tc.psum_pool(name="psum", bufs=1))
 
         offs_sb = keep.tile([P, S // 16], U16, name="offs_sb")
@@ -34,11 +35,15 @@ def tile_picked_yeditm_prob_p_kernel(
         words = keep.tile([P, T], U32, name="words", align_bytes=64)
         planes = keep.tile([P, T], U8, name="planes", align_bytes=64)
 
-        nc.gpsimd.memset(planes[:].bitcast(I32), 0)
+        nc.vector.memset(planes[:].bitcast(I32), 0)
+        warm_in = keep.tile([P, 1], F32, name="warm_in")
+        warm_out = keep.tile([P, 1], F32, name="warm_out")
+        nc.gpsimd.memset(warm_in[:], 1.0)
+        nc.scalar.activation(warm_out[:], warm_in[:], ACT.Ln)
         nc.sync.dma_start(offs_sb[:], offs)
         nc.sync.dma_start(words[:].bitcast(I32), x_words[0].rearrange("p n t -> p (n t)").bitcast(I32))
         for q in range(4):
-            nc.scalar.dma_start(
+            nc.sync.dma_start(
                 planes[32 * q : 32 * q + 4, :].bitcast(I32), x_scales[0, 4 * q : 4 * q + 4, :].bitcast(I32)
             )
 
@@ -46,7 +51,10 @@ def tile_picked_yeditm_prob_p_kernel(
             rows = w.rearrange("(p j) c -> p j c", j=PACK)
             halves = []
             for h in range(2):
-                raw = keep.tile([P, PACK, HALF], F32, name=f"{name}_raw{h}")
+                if (name, h) == ("w2", 1):
+                    raw = reuse.tile([P, PACK, HALF], F32, name=f"{name}_raw{h}", offset=4096)
+                else:
+                    raw = keep.tile([P, PACK, HALF], F32, name=f"{name}_raw{h}")
                 nc.sync.dma_start(raw[:], rows[:, :, h * HALF : (h + 1) * HALF])
                 halves.append(raw)
             return halves
@@ -66,8 +74,8 @@ def tile_picked_yeditm_prob_p_kernel(
 
         x_codes = keep.tile([P, S], U32, name="x_codes", align_bytes=64)
         x_plane = keep.tile([P, S], U8, name="x_plane", align_bytes=64)
-        nc.vector.tensor_copy(x_plane[:], planes[:].indirect(offs_sb[:]))
         nc.vector.tensor_copy(x_codes[:], words[:].indirect(offs_sb[:]))
+        nc.vector.tensor_copy(x_plane[:], planes[:].indirect(offs_sb[:]))
 
         def deal(copy, grouped, raw, h):
             m0 = h * HALF // PACK
@@ -105,40 +113,76 @@ def tile_picked_yeditm_prob_p_kernel(
         quantize(w1_codes, w1_plane, w1_bf, 1, 4)
         y_acc = [product(w1_codes, w1_plane, t, t) for t in range(PACK)]
 
-        w2_bf = keep.tile([P, PACK, P, PACK], BF16, name="w2_bf", align_bytes=64)
+        w2_bf = reuse.tile([P, PACK, P, PACK], BF16, name="w2_bf", align_bytes=64, offset=0)
         w2_codes = keep.tile([P, H], U32, name="w2_codes", align_bytes=64)
         w2_plane = keep.tile([P, H], U8, name="w2_plane", align_bytes=64)
-        deal(nc.scalar.copy, w2_bf, w2_raw[0], 0)
-
-        y = [keep.tile([P, S], F32, name=f"y{t}") for t in range(PACK)]
-        yv = [keep.tile([P, S], F32, name=f"yv{t}") for t in range(PACK)]
-        key = keep.tile([P, PACK, V], F32, name="key")
-        sq = keep.tile([P, PACK, PACK, V // PACK], F32, name="sq")
-        lg = keep.tile([P, PACK, V], F32, name="lg")
-        num = keep.tile([P, PACK, V], F32, name="num")
-        miss = keep.tile([P, PACK, V], F32, name="miss")
-
-        def keys(t):
-            sq_t = sq[:, t].rearrange("p c v -> p (c v)")
-            nc.scalar.copy(y[t][:], y_acc[t][:])
-            if t == 0:
-                nc.vector.tensor_copy(key[:, t, :], y[t][:].indirect(ed_sb[:]))
-                nc.vector.tensor_tensor(sq_t, key[:, t, :], key[:, t, :], ALU.mult)
-            else:
-                nc.scalar.activation(key[:, t, :], y[t][:].indirect(ed_sb[:]), ACT.Copy)
-                nc.scalar.activation(sq_t, key[:, t, :], ACT.Square)
-            nc.scalar.activation(lg[:, t, :], sq_t, ACT.Ln, bias=0.6)
-
-        keys(0)
+        deal(nc.vector.tensor_copy, w2_bf, w2_raw[0], 0)
         deal(nc.vector.tensor_copy, w2_bf, w2_raw[1], 1)
         quantize(w2_codes, w2_plane, w2_bf, 0, 4)
         yv_acc = [product(w2_codes, w2_plane, t, PACK + t) for t in range(PACK)]
-        for t in range(1, PACK):
-            keys(t)
+
+        y = [keep.tile([P, S], F32, name=f"y{t}") for t in range(2)]
+        y += [reuse.tile([P, S], F32, name=f"y{t}", offset=2048 * (t - 2)) for t in range(2, PACK)]
+        key = keep.tile([P, PACK, V], F32, name="key")
+        sq = keep.tile([P, PACK, PACK, V // PACK], F32, name="sq")
+        lg = [keep.tile([P, V], F32, name=f"lg{t}") for t in range(PACK)]
+        num = reuse.tile([P, PACK, V], F32, name="num", offset=4096)
+        miss = keep.tile([P, PACK, V], F32, name="miss")
+        match = keep.tile([P, PACK, V], F32, name="match")
+        bound = keep.tile([P, PACK, V], F32, name="bound")
+        delta = keep.tile([P, PACK, V], F32, name="delta")
+        vn = keep.tile([P, PACK, V], F32, name="vn")
+        hid = keep.tile([P, PACK, S], BF16, name="hid")
+
+        for t in range(PACK):
+            sq_t = sq[:, t].rearrange("p c v -> p (c v)")
+            if t < 2:
+                nc.scalar.copy(y[t][:], y_acc[t][:])
+                nc.scalar.activation(key[:, t, :], y[t][:].indirect(ed_sb[:]), ACT.Copy)
+            else:
+                nc.vector.tensor_copy(y[t][:], y_acc[t][:])
+                nc.vector.tensor_copy(key[:, t, :], y[t][:].indirect(ed_sb[:]))
+            nc.scalar.activation(sq_t, key[:, t, :], ACT.Square)
+            nc.scalar.activation(lg[t][:], sq_t, ACT.Ln, bias=0.6)
         for t in range(PACK):
             nc.vector.tensor_tensor(num[:, t, :], y[t][:].indirect(hit_sb[:]), key[:, t, :], ALU.mult)
-            nc.vector.tensor_copy(yv[t][:], yv_acc[t][:])
+        yv = [keep.tile([P, S], F32, name=f"yv{t}") for t in range(PACK)]
+
+        def residual(t):
+            nc.scalar.copy(yv[t][:], yv_acc[t][:])
             nc.vector.tensor_tensor(miss[:, t, :], yv[t][:].indirect(ed_sb[:]), tgt_sb[:, t, :], ALU.subtract)
+
+        def bounded_match(t):
+            rec_t = sq[:, :, t, :]
+            nc.scalar.activation(rec_t, lg[t][:].rearrange("p (c v) -> p c v", c=PACK), ACT.Exp, scale=-1.0)
+            nc.vector.tensor_tensor(
+                match[:, t, :].rearrange("p (c v) -> p c v", c=PACK),
+                num[:, t, :].rearrange("p (c v) -> p c v", c=PACK),
+                rec_t,
+                ALU.mult,
+            )
+            nc.scalar.activation(bound[:, t, :], match[:, t, :], ACT.Tanh)
+
+        def edit(t):
+            if t == 2:
+                nc.scalar.activation(vn[:, t, :], yv[t][:].indirect(hit_sb[:]), ACT.Copy)
+            nc.vector.scalar_tensor_tensor(delta[:, t, :], bound[:, t, :], -0.9, miss[:, t, :], ALU.mult, ALU.mult)
+            if t == 2:
+                nc.vector.tensor_tensor(yv[t][:].indirect(hit_sb[:]), vn[:, t, :], delta[:, t, :], ALU.add)
+            else:
+                nc.vector.tensor_tensor(vn[:, t, :], yv[t][:].indirect(hit_sb[:]), delta[:, t, :], ALU.add)
+                nc.scalar.activation(yv[t][:].indirect(hit_sb[:]), vn[:, t, :], ACT.Copy)
+
+        residual(0)
+        residual(1)
+        for t in range(PACK):
+            bounded_match(t)
+        edit(0)
+        residual(2)
+        edit(1)
+        residual(3)
+        edit(2)
+        edit(3)
 
         w3_bf = keep.tile([P, N, PACK], BF16, name="w3_bf", align_bytes=64)
         w3_codes = keep.tile([P, N], U32, name="w3_codes", align_bytes=64)
@@ -150,57 +194,29 @@ def tile_picked_yeditm_prob_p_kernel(
             out=w3_codes[:].bitcast(FP8X4), scales=w3_plane[:], in_=w3_bf[:].rearrange("p c j -> p (c j)")
         )
 
-        match = keep.tile([P, PACK, V], F32, name="match")
-        bound = keep.tile([P, PACK, V], F32, name="bound")
-        delta = keep.tile([P, PACK, V], F32, name="delta")
-        vn = keep.tile([P, PACK, V], F32, name="vn")
-        hid = keep.tile([P, PACK, S], BF16, name="hid")
-
-        def bounded_match(t):
-            rec_t = sq[:, :, t, :]
-            nc.scalar.activation(rec_t, lg[:, t, :].rearrange("p (c v) -> p c v", c=PACK), ACT.Exp, scale=-1.0)
-            nc.vector.tensor_tensor(
-                match[:, t, :].rearrange("p (c v) -> p c v", c=PACK),
-                num[:, t, :].rearrange("p (c v) -> p c v", c=PACK),
-                rec_t,
-                ALU.mult,
-            )
-            nc.scalar.activation(bound[:, t, :], match[:, t, :], ACT.Tanh)
-
-        def edit_store(t):
-            nc.vector.scalar_tensor_tensor(delta[:, t, :], bound[:, t, :], -0.9, miss[:, t, :], ALU.mult, ALU.mult)
-            if t < PACK - 1:
-                nc.vector.tensor_tensor(vn[:, t, :], yv[t][:].indirect(hit_sb[:]), delta[:, t, :], ALU.add)
-                nc.scalar.activation(yv[t][:].indirect(hit_sb[:]), vn[:, t, :], ACT.Copy)
-            else:
-                nc.scalar.activation(vn[:, t, :], yv[t][:].indirect(hit_sb[:]), ACT.Copy)
-                nc.vector.tensor_tensor(yv[t][:].indirect(hit_sb[:]), vn[:, t, :], delta[:, t, :], ALU.add)
-
-        def read_store(t):
-            nc.vector.scalar_tensor_tensor(
-                hid[:, t, :], yv[t][:], unit_sb[:, t : t + 1], probe_sb[:, t, :], ALU.mult, ALU.mult
-            )
-
+        pieces = 4
+        width = S // pieces
         for t in range(PACK):
-            bounded_match(t)
-        for t in range(PACK):
-            edit_store(t)
-        for t in range(PACK):
-            read_store(t)
+            step = S if t < PACK - 1 else width
+            for c0 in range(0, S, step):
+                cols = slice(c0, c0 + step)
+                nc.vector.scalar_tensor_tensor(
+                    hid[:, t, cols], yv[t][:, cols], unit_sb[:, t : t + 1], probe_sb[:, t, cols], ALU.mult, ALU.mult
+                )
 
         hid_bf = keep.tile([P, S, PACK], BF16, name="hid_bf", align_bytes=64)
         hid_codes = keep.tile([P, S], U32, name="hid_codes", align_bytes=64)
         hid_plane = keep.tile([P, S], U8, name="hid_plane", align_bytes=64)
         result = keep.tile([P, S], F32, name="result")
-        half = S // 2
-        for h, copy in ((0, nc.scalar.copy), (1, nc.vector.tensor_copy)):
-            cols = slice(h * half, (h + 1) * half)
+        for h in range(pieces):
+            cols = slice(h * width, (h + 1) * width)
+            copy = nc.vector.tensor_copy if h % 2 == 0 else nc.scalar.copy
             copy(
                 hid_bf[:, cols, :].rearrange("p (c i) t -> p c t i", i=4),
                 hid[:, :, cols].rearrange("p t (c i) -> p c t i", i=4),
             )
-        for h, copy in ((1, nc.scalar.copy), (0, nc.vector.tensor_copy)):
-            cols = slice(h * half, (h + 1) * half)
+        for h in range(pieces):
+            cols = slice(h * width, (h + 1) * width)
             nc.vector.quantize_mx(
                 out=hid_codes[:, cols].bitcast(FP8X4),
                 scales=hid_plane[:, cols],
@@ -208,7 +224,7 @@ def tile_picked_yeditm_prob_p_kernel(
             )
             acc = psum.tile([P, S], F32, name=f"bank{h}")
             nc.tensor.matmul_mx(
-                out=acc[:, :half],
+                out=acc[:, :width],
                 lhsT=w3_codes[:].bitcast(FP8X4),
                 lhsT_scale=w3_plane[:],
                 rhs=hid_codes[:, cols].bitcast(FP8X4),
@@ -216,5 +232,5 @@ def tile_picked_yeditm_prob_p_kernel(
                 start=True,
                 stop=True,
             )
-            copy(result[:, cols], acc[:, :half])
+            nc.scalar.copy(result[:, cols], acc[:, :width])
             nc.sync.dma_start(out[:, cols], result[:, cols])

from contextlib import ExitStack

import concourse.mybir as mybir

K, T, S, N, H, V = 512, 1024, 512, 128, 512, 256
FLOPS = 2 * K * H * S * 2 + 2 * H * N * S

F32 = mybir.dt.float32
BF16 = mybir.dt.bfloat16
I32 = mybir.dt.int32
U32 = mybir.dt.uint32
U16 = mybir.dt.uint16
U8 = mybir.dt.uint8
FP8X4 = mybir.dt.float8_e4m3fn_x4
ACT = mybir.ActivationFunctionType
ALU = mybir.AluOpType

P = 128
PACK = 4
HALF = H // 2


def tile_picked_yeditm_prob_p_kernel(
    tc, x_words, x_scales, w1, w2, tgt, probe, unit, w3, offs, ed, hit, out
):
    nc = tc.nc
    with ExitStack() as ctx:
        keep = ctx.enter_context(tc.tile_pool(name="keep", bufs=1))
        reuse = ctx.enter_context(tc.tile_pool(name="reuse", bufs=1))
        psum = ctx.enter_context(tc.psum_pool(name="psum", bufs=1))

        offs_sb = keep.tile([P, S // 16], U16, name="offs_sb")
        ed_sb = keep.tile([P, V // 16], U16, name="ed_sb")
        hit_sb = keep.tile([P, V // 16], U16, name="hit_sb")
        words = keep.tile([P, T], U32, name="words", align_bytes=64)
        planes = keep.tile([P, T], U8, name="planes", align_bytes=64)

        nc.vector.memset(planes[:].bitcast(I32), 0)
        warm_in = keep.tile([P, 1], F32, name="warm_in")
        warm_out = keep.tile([P, 1], F32, name="warm_out")
        nc.gpsimd.memset(warm_in[:], 1.0)
        nc.scalar.activation(warm_out[:], warm_in[:], ACT.Ln)
        nc.sync.dma_start(offs_sb[:], offs)
        nc.sync.dma_start(words[:].bitcast(I32), x_words[0].rearrange("p n t -> p (n t)").bitcast(I32))
        for q in range(4):
            nc.sync.dma_start(
                planes[32 * q : 32 * q + 4, :].bitcast(I32), x_scales[0, 4 * q : 4 * q + 4, :].bitcast(I32)
            )

        def load_halves(w, name):
            rows = w.rearrange("(p j) c -> p j c", j=PACK)
            halves = []
            for h in range(2):
                if (name, h) == ("w2", 1):
                    raw = reuse.tile([P, PACK, HALF], F32, name=f"{name}_raw{h}", offset=4096)
                else:
                    raw = keep.tile([P, PACK, HALF], F32, name=f"{name}_raw{h}")
                nc.sync.dma_start(raw[:], rows[:, :, h * HALF : (h + 1) * HALF])
                halves.append(raw)
            return halves

        w1_raw = load_halves(w1, "w1")
        nc.sync.dma_start(ed_sb[:], ed)
        nc.sync.dma_start(hit_sb[:], hit)
        w2_raw = load_halves(w2, "w2")
        tgt_sb = keep.tile([P, PACK, V], F32, name="tgt_sb")
        nc.sync.dma_start(tgt_sb[:], tgt.rearrange("(p t) v -> p t v", t=PACK))
        w3_raw = keep.tile([P, PACK, N], F32, name="w3_raw")
        nc.sync.dma_start(w3_raw[:], w3.rearrange("(p j) c -> p j c", j=PACK))
        unit_sb = keep.tile([P, PACK], F32, name="unit_sb")
        nc.sync.dma_start(unit_sb[:], unit.rearrange("(p t) o -> p (t o)", t=PACK))
        probe_sb = keep.tile([P, PACK, S], F32, name="probe_sb")
        nc.sync.dma_start(probe_sb[:], probe.rearrange("(p t) s -> p t s", t=PACK))

        x_codes = keep.tile([P, S], U32, name="x_codes", align_bytes=64)
        x_plane = keep.tile([P, S], U8, name="x_plane", align_bytes=64)
        nc.vector.tensor_copy(x_codes[:], words[:].indirect(offs_sb[:]))
        nc.vector.tensor_copy(x_plane[:], planes[:].indirect(offs_sb[:]))

        def deal(copy, grouped, raw, h):
            m0 = h * HALF // PACK
            copy(
                grouped[:, :, m0 : m0 + HALF // PACK, :].rearrange("p t m j -> p m j t"),
                raw[:].rearrange("p j (m t) -> p m j t", t=PACK),
            )

        def quantize(codes, plane, grouped, t0, t1):
            nc.vector.quantize_mx(
                out=codes[:, t0 * P : t1 * P].bitcast(FP8X4),
                scales=plane[:, t0 * P : t1 * P],
                in_=grouped[:, t0:t1].rearrange("p t m j -> p (t m j)"),
            )

        def product(codes, plane, t, bank):
            acc = psum.tile([P, S], F32, name=f"bank{bank}")
            nc.tensor.matmul_mx(
                out=acc[:],
                lhsT=codes[:, t * P : (t + 1) * P].bitcast(FP8X4),
                lhsT_scale=plane[:, t * P : (t + 1) * P],
                rhs=x_codes[:].bitcast(FP8X4),
                rhs_scale=x_plane[:],
                start=True,
                stop=True,
            )
            return acc

        w1_bf = keep.tile([P, PACK, P, PACK], BF16, name="w1_bf", align_bytes=64)
        w1_codes = keep.tile([P, H], U32, name="w1_codes", align_bytes=64)
        w1_plane = keep.tile([P, H], U8, name="w1_plane", align_bytes=64)
        deal(nc.scalar.copy, w1_bf, w1_raw[0], 0)
        deal(nc.vector.tensor_copy, w1_bf, w1_raw[1], 1)
        quantize(w1_codes, w1_plane, w1_bf, 0, 1)
        quantize(w1_codes, w1_plane, w1_bf, 1, 4)
        y_acc = [product(w1_codes, w1_plane, t, t) for t in range(PACK)]

        w2_bf = reuse.tile([P, PACK, P, PACK], BF16, name="w2_bf", align_bytes=64, offset=0)
        w2_codes = keep.tile([P, H], U32, name="w2_codes", align_bytes=64)
        w2_plane = keep.tile([P, H], U8, name="w2_plane", align_bytes=64)
        deal(nc.vector.tensor_copy, w2_bf, w2_raw[0], 0)
        deal(nc.vector.tensor_copy, w2_bf, w2_raw[1], 1)
        quantize(w2_codes, w2_plane, w2_bf, 0, 4)
        yv_acc = [product(w2_codes, w2_plane, t, PACK + t) for t in range(PACK)]

        y = [keep.tile([P, S], F32, name=f"y{t}") for t in range(2)]
        y += [reuse.tile([P, S], F32, name=f"y{t}", offset=2048 * (t - 2)) for t in range(2, PACK)]
        key = keep.tile([P, PACK, V], F32, name="key")
        sq = keep.tile([P, PACK, PACK, V // PACK], F32, name="sq")
        lg = [keep.tile([P, V], F32, name=f"lg{t}") for t in range(PACK)]
        num = reuse.tile([P, PACK, V], F32, name="num", offset=4096)
        miss = keep.tile([P, PACK, V], F32, name="miss")
        match = keep.tile([P, PACK, V], F32, name="match")
        bound = keep.tile([P, PACK, V], F32, name="bound")
        delta = keep.tile([P, PACK, V], F32, name="delta")
        vn = keep.tile([P, PACK, V], F32, name="vn")
        hid = keep.tile([P, PACK, S], BF16, name="hid")

        for t in range(PACK):
            sq_t = sq[:, t].rearrange("p c v -> p (c v)")
            if t < 2:
                nc.scalar.copy(y[t][:], y_acc[t][:])
                nc.scalar.activation(key[:, t, :], y[t][:].indirect(ed_sb[:]), ACT.Copy)
            else:
                nc.vector.tensor_copy(y[t][:], y_acc[t][:])
                nc.vector.tensor_copy(key[:, t, :], y[t][:].indirect(ed_sb[:]))
            nc.scalar.activation(sq_t, key[:, t, :], ACT.Square)
            nc.scalar.activation(lg[t][:], sq_t, ACT.Ln, bias=0.6)
        for t in range(PACK):
            nc.vector.tensor_tensor(num[:, t, :], y[t][:].indirect(hit_sb[:]), key[:, t, :], ALU.mult)
        yv = [keep.tile([P, S], F32, name=f"yv{t}") for t in range(PACK)]

        def residual(t):
            nc.scalar.copy(yv[t][:], yv_acc[t][:])
            nc.vector.tensor_tensor(miss[:, t, :], yv[t][:].indirect(ed_sb[:]), tgt_sb[:, t, :], ALU.subtract)

        def bounded_match(t):
            rec_t = sq[:, :, t, :]
            nc.scalar.activation(rec_t, lg[t][:].rearrange("p (c v) -> p c v", c=PACK), ACT.Exp, scale=-1.0)
            nc.vector.tensor_tensor(
                match[:, t, :].rearrange("p (c v) -> p c v", c=PACK),
                num[:, t, :].rearrange("p (c v) -> p c v", c=PACK),
                rec_t,
                ALU.mult,
            )
            nc.scalar.activation(bound[:, t, :], match[:, t, :], ACT.Tanh)

        def edit(t):
            if t == 2:
                nc.scalar.activation(vn[:, t, :], yv[t][:].indirect(hit_sb[:]), ACT.Copy)
            nc.vector.scalar_tensor_tensor(delta[:, t, :], bound[:, t, :], -0.9, miss[:, t, :], ALU.mult, ALU.mult)
            if t == 2:
                nc.vector.tensor_tensor(yv[t][:].indirect(hit_sb[:]), vn[:, t, :], delta[:, t, :], ALU.add)
            else:
                nc.vector.tensor_tensor(vn[:, t, :], yv[t][:].indirect(hit_sb[:]), delta[:, t, :], ALU.add)
                nc.scalar.activation(yv[t][:].indirect(hit_sb[:]), vn[:, t, :], ACT.Copy)

        residual(0)
        residual(1)
        for t in range(PACK):
            bounded_match(t)
        edit(0)
        residual(2)
        edit(1)
        residual(3)
        edit(2)
        edit(3)

        w3_bf = keep.tile([P, N, PACK], BF16, name="w3_bf", align_bytes=64)
        w3_codes = keep.tile([P, N], U32, name="w3_codes", align_bytes=64)
        w3_plane = keep.tile([P, N], U8, name="w3_plane", align_bytes=64)
        nc.vector.tensor_copy(
            w3_bf[:].rearrange("p (c i) j -> p c j i", i=4), w3_raw[:].rearrange("p j (c i) -> p c j i", i=4)
        )
        nc.vector.quantize_mx(
            out=w3_codes[:].bitcast(FP8X4), scales=w3_plane[:], in_=w3_bf[:].rearrange("p c j -> p (c j)")
        )

        pieces = 4
        width = S // pieces
        for t in range(PACK):
            step = S if t < PACK - 1 else width
            for c0 in range(0, S, step):
                cols = slice(c0, c0 + step)
                nc.vector.scalar_tensor_tensor(
                    hid[:, t, cols], yv[t][:, cols], unit_sb[:, t : t + 1], probe_sb[:, t, cols], ALU.mult, ALU.mult
                )

        hid_bf = keep.tile([P, S, PACK], BF16, name="hid_bf", align_bytes=64)
        hid_codes = keep.tile([P, S], U32, name="hid_codes", align_bytes=64)
        hid_plane = keep.tile([P, S], U8, name="hid_plane", align_bytes=64)
        result = keep.tile([P, S], F32, name="result")
        for h in range(pieces):
            cols = slice(h * width, (h + 1) * width)
            copy = nc.vector.tensor_copy if h % 2 == 0 else nc.scalar.copy
            copy(
                hid_bf[:, cols, :].rearrange("p (c i) t -> p c t i", i=4),
                hid[:, :, cols].rearrange("p t (c i) -> p c t i", i=4),
            )
        for h in range(pieces):
            cols = slice(h * width, (h + 1) * width)
            nc.vector.quantize_mx(
                out=hid_codes[:, cols].bitcast(FP8X4),
                scales=hid_plane[:, cols],
                in_=hid_bf[:, cols, :].rearrange("p c t -> p (c t)"),
            )
            acc = psum.tile([P, S], F32, name=f"bank{h}")
            nc.tensor.matmul_mx(
                out=acc[:, :width],
                lhsT=w3_codes[:].bitcast(FP8X4),
                lhsT_scale=w3_plane[:],
                rhs=hid_codes[:, cols].bitcast(FP8X4),
                rhs_scale=hid_plane[:, cols],
                start=True,
                stop=True,
            )
            nc.scalar.copy(result[:, cols], acc[:, :width])
            nc.sync.dma_start(out[:, cols], result[:, cols])
